import numpy as np
import ml_dtypes


def mxq(x, axis, fmt="e4m3"):
    dtype, down = {"e4m3": (ml_dtypes.float8_e4m3fn, 7), "e5m2": (ml_dtypes.float8_e5m2, 14)}[fmt]
    v = np.moveaxis(np.asarray(x, np.float32).astype(ml_dtypes.bfloat16).astype(np.float64), axis, -1)
    blocks = v.reshape(v.shape[:-1] + (-1, 32))
    amax = np.abs(blocks).max(-1, keepdims=True)
    byte = np.maximum(np.where(amax > 0, np.frexp(amax)[1] - 1 + 127, 0) - down, 1)
    scale = np.exp2(byte - 127.0)
    codes = (blocks / scale).astype(np.float32).astype(dtype).astype(np.float64)
    return np.moveaxis((codes * scale).reshape(v.shape), -1, axis)


WIDE = False


def mx_kscale(k):
    if not WIDE:
        return np.ones(k)
    levels = np.array([10, -10, 5, -5, 0])
    if k % 512:
        return np.exp2(np.random.permutation(np.resize(levels, k // 32))).repeat(32)
    a = np.empty((k // 512, 16))
    for p in range(k // 512):
        a[p, :8] = np.random.permutation(np.resize(levels, 8))
        for g in range(8):
            far = levels[np.abs(levels - a[p, g]) >= 10]
            a[p, g + 8] = far[np.random.randint(len(far))]
    return np.exp2(a.ravel()).repeat(32)


def f64(x):
    return np.asarray(x).astype(np.float64)


def striped8(idx):
    return np.asarray(idx).reshape(8, -1, 16).transpose(0, 2, 1).reshape(128, -1).astype(np.uint16)


def unstriped8(offs):
    return offs.reshape(8, 16, -1).transpose(0, 2, 1).reshape(8, -1).astype(np.int64)


def pick8(x, idx, run):
    r = np.arange(len(x))
    return x[r[:, None], idx[r % (8 * run) // run]]


E2M1 = np.array([0.0, 0.5, 1.0, 1.5, 2.0, 3.0, 4.0, 6.0, -0.0, -0.5, -1.0, -1.5, -2.0, -3.0, -4.0, -6.0])


def pack_weight(w, fmt):
    k, n = w.shape
    w = f64(np.asarray(w, np.float32).astype(ml_dtypes.bfloat16)).reshape(k // 32, 32, n)
    amax = np.abs(w).max(1)
    if fmt == "e4m3":
        byte = np.frexp(amax)[1] - 1 + 127 - 7
    else:
        mant, ex = np.frexp(amax / 6.0)
        byte = np.where(mant > 0.5, ex, ex - 1) + 127
    byte = np.clip(np.where(amax > 0, byte, 1), 1, 254)
    scaled = (w * np.exp2(127.0 - byte)[:, None, :]).reshape(k, n).astype(np.float32)
    by_word = np.ascontiguousarray(scaled.reshape(k // 512, 128, 4, n).transpose(0, 1, 3, 2))
    if fmt == "e4m3":
        words = by_word.astype(ml_dtypes.float8_e4m3fn).view(np.uint8)
    else:
        c = by_word.astype(ml_dtypes.float4_e2m1fn).view(np.uint8) & 0xF
        words = (c[..., 0::2] | (c[..., 1::2] << 4)).reshape(k // 512, 128, 2 * n)
    return np.ascontiguousarray(words), np.ascontiguousarray(byte.astype(np.uint8).reshape(k // 512, 16, n))


def unpack_weight(words, scales, fmt):
    g, _, n = scales.shape
    words = np.ascontiguousarray(words).reshape(g, 128, n, -1)
    if fmt == "e4m3":
        vals = words.view(ml_dtypes.float8_e4m3fn).astype(np.float64)
    else:
        nib = np.empty((g, 128, n, 4), np.uint8)
        nib[..., 0::2] = words & 0xF
        nib[..., 1::2] = words >> 4
        vals = E2M1[nib]
    vals = vals * np.repeat(np.exp2(scales.astype(np.float64) - 127.0), 8, axis=1)[..., None]
    return vals.transpose(0, 1, 3, 2).reshape(g * 512, n)


def sigmoid(v):
    return 1.0 / (1.0 + np.exp(-v))


D, T, U, Z, I, Q = 512, 1024, 1024, 1024, 512, 128


def setup_inputs():
    n = np.random.standard_normal
    idx = np.stack([np.random.permutation(T)[:I] for _ in range(8)])
    idx2 = np.stack([np.random.permutation(U)[:I] for _ in range(8)])
    idx3 = np.stack([np.random.permutation(Z)[:I] for _ in range(8)])
    idx4 = np.stack([np.random.permutation(Z)[:I] for _ in range(8)])
    idx5 = np.stack([np.random.permutation(Z)[:I] for _ in range(8)])
    fd = mx_kscale(D)
    keysp = pack_weight(n((D, T)) / fd[:, None], "e4m3")
    notesp = pack_weight(n((D, U)) / fd[:, None], "e2m1")
    return {
        "query": (n((D, Q)) * 1.0 / np.sqrt(D) * fd[:, None]).astype(np.float32),
        "keys_words": keysp[0],
        "keys_scales": keysp[1],
        "notes_words": notesp[0],
        "notes_scales": notesp[1],
        "thr": (np.random.uniform(-0.6, 0.6, (Q, 1))).astype(np.float32),
        "slope": (np.random.uniform(1.0, 3.0, (Q, 1))).astype(np.float32),
        "old": (1.0 * n((Q, Z))).astype(np.float32),
        "offs": striped8(idx),
        "offs2": striped8(idx2),
        "offs3": striped8(idx3),
        "offs4": striped8(idx4),
        "offs5": striped8(idx5),
    }


def reference(query, keys_words, keys_scales, notes_words, notes_scales, thr, slope, old, offs, offs2, offs3, offs4, offs5):
    idx = unstriped8(offs)
    idx2 = unstriped8(offs2)
    idx3 = unstriped8(offs3)
    idx4 = unstriped8(offs4)
    idx5 = unstriped8(offs5)
    keysu = unpack_weight(keys_words, keys_scales, "e4m3")
    notesu = unpack_weight(notes_words, notes_scales, "e2m1")
    queryq = mxq(f64(query), 0, "e4m3")
    a = queryq.T @ keysu
    b = queryq.T @ notesu
    s1 = sigmoid(pick8(a, idx, 16) * f64(slope) + f64(thr))
    s2 = sigmoid(pick8(b, idx2, 16) * f64(slope) + f64(thr))
    f1 = np.zeros((Q, Z))
    f1[np.arange(Q)[:, None], idx3[np.arange(Q) % 128 // 16]] = s1
    f2 = np.zeros((Q, Z))
    f2[np.arange(Q)[:, None], idx4[np.arange(Q) % 128 // 16]] = s2
    r = f1 - f2
    cc = f64(old) + r
    y = pick8(cc, idx5, 16)
    return y

@@ -1,0 +1,159 @@
+from contextlib import ExitStack
+
+import concourse.mybir as mybir
+from concourse.masks import make_identity
+
+D, T, Z, SLOTS, Q = 512, 1024, 1024, 512, 128
+FLOPS = 2 * 2 * D * Q * T
+
+F32 = mybir.dt.float32
+BF16 = mybir.dt.bfloat16
+I32 = mybir.dt.int32
+U32 = mybir.dt.uint32
+U16 = mybir.dt.uint16
+U8 = mybir.dt.uint8
+FP8X4 = mybir.dt.float8_e4m3fn_x4
+FP4X4 = mybir.dt.float4_e2m1fn_x4
+ACT = mybir.ActivationFunctionType
+ALU = mybir.AluOpType
+
+P = 128
+PACK = 4
+BANK = 512
+HALF = SLOTS // 2
+LIST_COLS = SLOTS // 16
+A_PIECES = (256, 256, 256, 128, 128)
+TURN = 256
+
+
+def tile_attend_twogates_two_kernel(tc, query, keys_words, keys_scales, notes_words, notes_scales,
+                                     thr, slope, old, offs, offs2, offs3, offs4, offs5, out):
+    nc = tc.nc
+    with ExitStack() as ctx:
+        lists = ctx.enter_context(tc.tile_pool(name="lists", bufs=1))
+        keep = ctx.enter_context(tc.tile_pool(name="keep", bufs=1))
+        psum = ctx.enter_context(tc.psum_pool(name="psum", bufs=1))
+
+        def load_list(src, name):
+            t = lists.tile([P, LIST_COLS], U16, name=name)
+            nc.sync.dma_start(t[:], src)
+            return t
+
+        def load_plane(queue, scales, name):
+            plane = keep.tile([P, T], U8, name=name, align_bytes=64)
+            for r in range(4):
+                queue.dma_start(plane[r:P:32, :].bitcast(I32), scales[0, r:16:4, :].bitcast(I32))
+            return plane
+
+        def half(offsets, h):
+            return offsets[:, h * LIST_COLS // 2:(h + 1) * LIST_COLS // 2]
+
+        def bank(b, name):
+            return psum.tile([P, BANK], F32, name=name, tag="bank%d" % b)
+
+        q_raw = keep.tile([P, PACK, Q], F32, name="q_raw")
+        nc.sync.dma_start(q_raw[:], query.rearrange("(p j) q -> p j q", j=PACK))
+        k_plane = load_plane(nc.sync, keys_scales, "k_plane")
+        kw_dram = keys_words[0].rearrange("p n t -> p (n t)").bitcast(I32)
+        k_words = []
+        for h in range(2):
+            kw = keep.tile([P, T // 2], I32, name="k_words%d" % h, align_bytes=64)
+            nc.sync.dma_start(kw[:], kw_dram[:, h * T // 2:(h + 1) * T // 2])
+            k_words.append(kw)
+        thr_sb = keep.tile([P, 1], F32, name="thr_sb")
+        slope_sb = keep.tile([P, 1], F32, name="slope_sb")
+        nc.sync.dma_start(slope_sb[:], slope)
+        nc.gpsimd.dma_start(thr_sb[:], thr)
+        idx = load_list(offs, "idx")
+        idx3 = load_list(offs3, "idx3")
+        n_words = keep.tile([P, 2 * T], U8, name="n_words", align_bytes=64)
+        nc.sync.dma_start(n_words[:].bitcast(I32), notes_words[0].bitcast(I32))
+        n_plane = load_plane(nc.sync, notes_scales, "n_plane")
+        idx2 = load_list(offs2, "idx2")
+        old_sb = keep.tile([P, Z], F32, name="old_sb")
+        nc.sync.dma_start(old_sb[:], old)
+        idx4 = load_list(offs4, "idx4")
+        idx5 = load_list(offs5, "idx5")
+
+        f1 = [keep.tile([P, Z], F32, name="f1_%d" % h) for h in range(2)]
+        nc.vector.memset(f1[0][:], 0.0)
+        nc.vector.memset(f1[1][:], 0.0)
+        ident = keep.tile([P, P], F32, name="ident")
+        make_identity(nc, ident[:])
+
+        q_bf = keep.tile([P, Q, PACK], BF16, name="q_bf", tag="q_then_f2", align_bytes=64)
+        q_codes = keep.tile([P, Q], U32, name="q_codes", align_bytes=64)
+        q_plane = keep.tile([P, Q], U8, name="q_plane", align_bytes=64)
+        q_halves = [slice(0, Q // 2), slice(Q // 2, Q)]
+        for cols in q_halves:
+            nc.vector.tensor_copy(q_bf[:, cols, :].rearrange("p (c i) j -> p c j i", i=4),
+                                  q_raw[:, :, cols].rearrange("p j (c i) -> p c j i", i=4))
+        for cols in q_halves:
+            nc.vector.quantize_mx(out=q_codes[:, cols].bitcast(FP8X4), scales=q_plane[:, cols],
+                                  in_=q_bf[:, cols, :].rearrange("p q j -> p (q j)"))
+        f2 = keep.tile([P, Z], F32, name="f2", tag="q_then_f2", align_bytes=64)
+        nc.gpsimd.memset(f2[:], 0.0)
+
+        a_sb = keep.tile([P, T], F32, name="a_sb", tag="rows")
+        c0 = 0
+        for b, width in enumerate(A_PIECES):
+            acc = bank(b, "a_acc%d" % b)
+            kw = k_words[c0 // (T // 2)]
+            w0 = c0 % (T // 2)
+            nc.tensor.matmul_mx(out=acc[:, :width], lhsT=q_codes[:].bitcast(FP8X4), lhsT_scale=q_plane[:],
+                                rhs=kw[:, w0:w0 + width].bitcast(FP8X4), rhs_scale=k_plane[:, c0:c0 + width],
+                                start=True, stop=True)
+            nc.vector.tensor_copy(a_sb[:, c0:c0 + width], acc[:, :width])
+            c0 = c0 + width
+
+        s1 = keep.tile([P, SLOTS], F32, name="s1")
+        for h in range(2):
+            cols = slice(h * HALF, (h + 1) * HALF)
+            nc.scalar.activation(s1[:, cols], a_sb[:].indirect(half(idx, h)), ACT.Sigmoid,
+                                 bias=thr_sb[:], scale=slope_sb[:])
+            nc.vector.tensor_copy(f1[h][:].indirect(half(idx3, h)), s1[:, cols])
+
+        b_sb = keep.tile([P, T], F32, name="b_sb", tag="rows")
+        for c in range(T // BANK):
+            cols = slice(c * BANK, (c + 1) * BANK)
+            acc = bank(c, "b_acc%d" % c)
+            nc.tensor.matmul_mx(out=acc[:], lhsT=q_codes[:].bitcast(FP8X4), lhsT_scale=q_plane[:],
+                                rhs=n_words[:, 2 * c * BANK:2 * (c + 1) * BANK].bitcast(FP4X4),
+                                rhs_scale=n_plane[:, cols], start=True, stop=True)
+            nc.scalar.copy(b_sb[:, cols], acc[:])
+
+        s2 = keep.tile([P, SLOTS], F32, name="s2")
+        for h in range(2):
+            cols = slice(h * HALF, (h + 1) * HALF)
+            nc.scalar.activation(s2[:, cols], b_sb[:].indirect(half(idx2, h)), ACT.Sigmoid,
+                                 bias=thr_sb[:], scale=slope_sb[:])
+            nc.vector.tensor_copy(f2[:].indirect(half(idx4, h)), s2[:, cols])
+
+        n_turn = Z // TURN
+        per = TURN // P
+        turned = [bank(8 - n_turn + g, "turned%d" % g) for g in range(n_turn)]
+        for n, src in enumerate((old_sb, f1[0], f1[1])):
+            for g in range(n_turn):
+                for j in range(per):
+                    z0 = g * TURN + j * P
+                    nc.tensor.matmul(turned[g][:, j * P:(j + 1) * P], lhsT=src[:, z0:z0 + P], rhs=ident[:],
+                                     is_transpose=True, start=(n == 0 and j == 0), stop=(n == 2 and j == per - 1))
+        raised_t = keep.tile([P, Z], F32, name="raised_t", tag="rows")
+        raised = [bank(2 + c, "raised%d" % c) for c in range(Z // BANK)]
+        for g in range(n_turn):
+            nc.scalar.copy(raised_t[:, g * TURN:(g + 1) * TURN], turned[g][:, :TURN])
+            for j in range(per):
+                z0 = g * TURN + j * P
+                nc.tensor.transpose(raised[z0 // BANK][:, z0 % BANK:z0 % BANK + P], raised_t[:, z0:z0 + P], ident[:])
+
+        cc = keep.tile([P, Z], F32, name="cc")
+        for c in range(Z // BANK):
+            cols = slice(c * BANK, (c + 1) * BANK)
+            nc.vector.tensor_tensor(cc[:, cols], raised[c][:], f2[:, cols], ALU.subtract)
+
+        y0 = keep.tile([P, HALF], F32, name="y0")
+        nc.vector.tensor_copy(y0[:], cc[:].indirect(half(idx5, 0)))
+        nc.sync.dma_start(out[:, :HALF], y0[:])
+        y1 = keep.tile([P, HALF], F32, name="y1")
+        nc.scalar.activation(y1[:], cc[:].indirect(half(idx5, 1)), ACT.Copy)
+        nc.scalar.dma_start(out[:, HALF:], y1[:])

@@ -75,6 +75,11 @@ def tile_attend_twogates_two_kernel(tc, query, keys_words, keys_scales, notes_wo
         idx4 = load_list(offs4, "idx4")
         idx5 = load_list(offs5, "idx5")
 
+        warm_in = keep.tile([P, 1], F32, name="warm_in")
+        warm_out = keep.tile([P, 1], F32, name="warm_out")
+        nc.vector.memset(warm_in[:], 0.0)
+        nc.scalar.activation(warm_out[:], warm_in[:], ACT.Sigmoid)
+
         f1 = [keep.tile([P, Z], F32, name="f1_%d" % h) for h in range(2)]
         nc.vector.memset(f1[0][:], 0.0)
         nc.vector.memset(f1[1][:], 0.0)

@@ -22,8 +22,9 @@ PACK = 4
 BANK = 512
 HALF = SLOTS // 2
 LIST_COLS = SLOTS // 16
-A_PIECES = (256, 256, 256, 128, 128)
+B_PIECES = (256, 256, 256, 128, 128)
 TURN = 256
+POOL_COLS = 224
 
 
 def tile_attend_twogates_two_kernel(tc, query, keys_words, keys_scales, notes_words, notes_scales,
@@ -39,10 +40,10 @@ def tile_attend_twogates_two_kernel(tc, query, keys_words, keys_scales, notes_wo
             nc.sync.dma_start(t[:], src)
             return t
 
-        def load_plane(queue, scales, name):
+        def load_plane(scales, name):
             plane = keep.tile([P, T], U8, name=name, align_bytes=64)
             for r in range(4):
-                queue.dma_start(plane[r:P:32, :].bitcast(I32), scales[0, r:16:4, :].bitcast(I32))
+                nc.sync.dma_start(plane[r:P:32, :].bitcast(I32), scales[0, r:16:4, :].bitcast(I32))
             return plane
 
         def half(offsets, h):
@@ -53,26 +54,22 @@ def tile_attend_twogates_two_kernel(tc, query, keys_words, keys_scales, notes_wo
 
         q_raw = keep.tile([P, PACK, Q], F32, name="q_raw")
         nc.sync.dma_start(q_raw[:], query.rearrange("(p j) q -> p j q", j=PACK))
-        k_plane = load_plane(nc.sync, keys_scales, "k_plane")
-        kw_dram = keys_words[0].rearrange("p n t -> p (n t)").bitcast(I32)
-        k_words = []
-        for h in range(2):
-            kw = keep.tile([P, T // 2], I32, name="k_words%d" % h, align_bytes=64)
-            nc.sync.dma_start(kw[:], kw_dram[:, h * T // 2:(h + 1) * T // 2])
-            k_words.append(kw)
+        n_plane = load_plane(notes_scales, "n_plane")
+        n_words = keep.tile([P, 2 * T], U8, name="n_words", align_bytes=64)
+        nc.sync.dma_start(n_words[:].bitcast(I32), notes_words[0].bitcast(I32))
         thr_sb = keep.tile([P, 1], F32, name="thr_sb")
         slope_sb = keep.tile([P, 1], F32, name="slope_sb")
         nc.sync.dma_start(slope_sb[:], slope)
-        nc.gpsimd.dma_start(thr_sb[:], thr)
-        idx = load_list(offs, "idx")
-        idx3 = load_list(offs3, "idx3")
-        n_words = keep.tile([P, 2 * T], U8, name="n_words", align_bytes=64)
-        nc.sync.dma_start(n_words[:].bitcast(I32), notes_words[0].bitcast(I32))
-        n_plane = load_plane(nc.sync, notes_scales, "n_plane")
+        nc.sync.dma_start(thr_sb[:], thr)
         idx2 = load_list(offs2, "idx2")
+        idx4 = load_list(offs4, "idx4")
+        k_words = keep.tile([P, T], I32, name="k_words", align_bytes=64)
+        nc.sync.dma_start(k_words[:], keys_words[0].rearrange("p n t -> p (n t)").bitcast(I32))
+        k_plane = load_plane(keys_scales, "k_plane")
+        idx = load_list(offs, "idx")
         old_sb = keep.tile([P, Z], F32, name="old_sb")
         nc.sync.dma_start(old_sb[:], old)
-        idx4 = load_list(offs4, "idx4")
+        idx3 = load_list(offs3, "idx3")
         idx5 = load_list(offs5, "idx5")
 
         warm_in = keep.tile([P, 1], F32, name="warm_in")
@@ -80,13 +77,15 @@ def tile_attend_twogates_two_kernel(tc, query, keys_words, keys_scales, notes_wo
         nc.vector.memset(warm_in[:], 0.0)
         nc.scalar.activation(warm_out[:], warm_in[:], ACT.Sigmoid)
 
-        f1 = [keep.tile([P, Z], F32, name="f1_%d" % h) for h in range(2)]
-        nc.vector.memset(f1[0][:], 0.0)
-        nc.vector.memset(f1[1][:], 0.0)
+        minus_f2 = [keep.tile([P, Z], F32, name="minus_f2_%d" % h) for h in range(2)]
+        minus_one = keep.tile([P, HALF], F32, name="minus_one")
+        nc.vector.memset(minus_f2[0][:], 0.0)
+        nc.vector.memset(minus_f2[1][:], 0.0)
+        nc.gpsimd.memset(minus_one[:], -1.0)
         ident = keep.tile([P, P], F32, name="ident")
         make_identity(nc, ident[:])
 
-        q_bf = keep.tile([P, Q, PACK], BF16, name="q_bf", tag="q_then_f2", align_bytes=64)
+        q_bf = keep.tile([P, Q, PACK], BF16, name="q_bf", tag="q_then_f1", align_bytes=64)
         q_codes = keep.tile([P, Q], U32, name="q_codes", align_bytes=64)
         q_plane = keep.tile([P, Q], U8, name="q_plane", align_bytes=64)
         q_halves = [slice(0, Q // 2), slice(Q // 2, Q)]
@@ -96,65 +95,66 @@ def tile_attend_twogates_two_kernel(tc, query, keys_words, keys_scales, notes_wo
         for cols in q_halves:
             nc.vector.quantize_mx(out=q_codes[:, cols].bitcast(FP8X4), scales=q_plane[:, cols],
                                   in_=q_bf[:, cols, :].rearrange("p q j -> p (q j)"))
-        f2 = keep.tile([P, Z], F32, name="f2", tag="q_then_f2", align_bytes=64)
-        nc.gpsimd.memset(f2[:], 0.0)
-
-        a_sb = keep.tile([P, T], F32, name="a_sb", tag="rows")
-        c0 = 0
-        for b, width in enumerate(A_PIECES):
-            acc = bank(b, "a_acc%d" % b)
-            kw = k_words[c0 // (T // 2)]
-            w0 = c0 % (T // 2)
-            nc.tensor.matmul_mx(out=acc[:, :width], lhsT=q_codes[:].bitcast(FP8X4), lhsT_scale=q_plane[:],
-                                rhs=kw[:, w0:w0 + width].bitcast(FP8X4), rhs_scale=k_plane[:, c0:c0 + width],
-                                start=True, stop=True)
-            nc.vector.tensor_copy(a_sb[:, c0:c0 + width], acc[:, :width])
-            c0 = c0 + width
-
-        s1 = keep.tile([P, SLOTS], F32, name="s1")
-        for h in range(2):
-            cols = slice(h * HALF, (h + 1) * HALF)
-            nc.scalar.activation(s1[:, cols], a_sb[:].indirect(half(idx, h)), ACT.Sigmoid,
-                                 bias=thr_sb[:], scale=slope_sb[:])
-            nc.vector.tensor_copy(f1[h][:].indirect(half(idx3, h)), s1[:, cols])
+        f1 = keep.tile([P, Z], F32, name="f1", tag="q_then_f1", align_bytes=64)
+        nc.gpsimd.memset(f1[:], 0.0)
 
         b_sb = keep.tile([P, T], F32, name="b_sb", tag="rows")
-        for c in range(T // BANK):
-            cols = slice(c * BANK, (c + 1) * BANK)
-            acc = bank(c, "b_acc%d" % c)
-            nc.tensor.matmul_mx(out=acc[:], lhsT=q_codes[:].bitcast(FP8X4), lhsT_scale=q_plane[:],
-                                rhs=n_words[:, 2 * c * BANK:2 * (c + 1) * BANK].bitcast(FP4X4),
-                                rhs_scale=n_plane[:, cols], start=True, stop=True)
-            nc.scalar.copy(b_sb[:, cols], acc[:])
+        c0 = 0
+        for n, width in enumerate(B_PIECES):
+            acc = bank(n, "b_acc%d" % n)
+            nc.tensor.matmul_mx(out=acc[:, :width], lhsT=q_codes[:].bitcast(FP8X4), lhsT_scale=q_plane[:],
+                                rhs=n_words[:, 2 * c0:2 * (c0 + width)].bitcast(FP4X4),
+                                rhs_scale=n_plane[:, c0:c0 + width], start=True, stop=True)
+            copy_out = nc.vector.tensor_copy if n % 2 == 0 else nc.scalar.copy
+            copy_out(b_sb[:, c0:c0 + width], acc[:, :width])
+            c0 = c0 + width
 
         s2 = keep.tile([P, SLOTS], F32, name="s2")
         for h in range(2):
             cols = slice(h * HALF, (h + 1) * HALF)
             nc.scalar.activation(s2[:, cols], b_sb[:].indirect(half(idx2, h)), ACT.Sigmoid,
                                  bias=thr_sb[:], scale=slope_sb[:])
-            nc.vector.tensor_copy(f2[:].indirect(half(idx4, h)), s2[:, cols])
+            nc.vector.tensor_tensor(minus_f2[h][:].indirect(half(idx4, h)), s2[:, cols], minus_one[:], ALU.mult)
+
+        a_sb = keep.tile([P, T], F32, name="a_sb", tag="rows")
+        for c in range(T // BANK):
+            cols = slice(c * BANK, (c + 1) * BANK)
+            acc = bank(c, "a_acc%d" % c)
+            nc.tensor.matmul_mx(out=acc[:], lhsT=q_codes[:].bitcast(FP8X4), lhsT_scale=q_plane[:],
+                                rhs=k_words[:, cols].bitcast(FP8X4), rhs_scale=k_plane[:, cols],
+                                start=True, stop=True)
+            nc.scalar.copy(a_sb[:, cols], acc[:])
+
+        s1 = keep.tile([P, SLOTS], F32, name="s1")
+        for h in range(2):
+            cols = slice(h * HALF, (h + 1) * HALF)
+            nc.scalar.activation(s1[:, cols], a_sb[:].indirect(half(idx, h)), ACT.Sigmoid,
+                                 bias=thr_sb[:], scale=slope_sb[:])
+            nc.vector.tensor_copy(f1[:].indirect(half(idx3, h)), s1[:, cols])
 
         n_turn = Z // TURN
         per = TURN // P
         turned = [bank(8 - n_turn + g, "turned%d" % g) for g in range(n_turn)]
-        for n, src in enumerate((old_sb, f1[0], f1[1])):
+        for n, src in enumerate((old_sb, minus_f2[0], minus_f2[1])):
             for g in range(n_turn):
                 for j in range(per):
                     z0 = g * TURN + j * P
                     nc.tensor.matmul(turned[g][:, j * P:(j + 1) * P], lhsT=src[:, z0:z0 + P], rhs=ident[:],
                                      is_transpose=True, start=(n == 0 and j == 0), stop=(n == 2 and j == per - 1))
-        raised_t = keep.tile([P, Z], F32, name="raised_t", tag="rows")
-        raised = [bank(2 + c, "raised%d" % c) for c in range(Z // BANK)]
+        lowered_t = keep.tile([P, Z], F32, name="lowered_t", tag="rows")
+        lowered = [bank(2 + c, "lowered%d" % c) for c in range(Z // BANK)]
         for g in range(n_turn):
-            nc.scalar.copy(raised_t[:, g * TURN:(g + 1) * TURN], turned[g][:, :TURN])
+            nc.scalar.copy(lowered_t[:, g * TURN:(g + 1) * TURN], turned[g][:, :TURN])
             for j in range(per):
                 z0 = g * TURN + j * P
-                nc.tensor.transpose(raised[z0 // BANK][:, z0 % BANK:z0 % BANK + P], raised_t[:, z0:z0 + P], ident[:])
+                nc.tensor.transpose(lowered[z0 // BANK][:, z0 % BANK:z0 % BANK + P], lowered_t[:, z0:z0 + P], ident[:])
 
         cc = keep.tile([P, Z], F32, name="cc")
-        for c in range(Z // BANK):
-            cols = slice(c * BANK, (c + 1) * BANK)
-            nc.vector.tensor_tensor(cc[:, cols], raised[c][:], f2[:, cols], ALU.subtract)
+        lowered_head = keep.tile([P, POOL_COLS], F32, name="lowered_head")
+        nc.scalar.copy(lowered_head[:], lowered[0][:, :POOL_COLS])
+        nc.gpsimd.tensor_tensor(cc[:, :POOL_COLS], lowered_head[:], f1[:, :POOL_COLS], ALU.add)
+        nc.vector.tensor_tensor(cc[:, POOL_COLS:BANK], lowered[0][:, POOL_COLS:], f1[:, POOL_COLS:BANK], ALU.add)
+        nc.vector.tensor_tensor(cc[:, BANK:], lowered[1][:], f1[:, BANK:], ALU.add)
 
         y0 = keep.tile([P, HALF], F32, name="y0")
         nc.vector.tensor_copy(y0[:], cc[:].indirect(half(idx5, 0)))

@@ -57,18 +57,20 @@ def tile_attend_twogates_two_kernel(tc, query, keys_words, keys_scales, notes_wo
         n_plane = load_plane(notes_scales, "n_plane")
         n_words = keep.tile([P, 2 * T], U8, name="n_words", align_bytes=64)
         nc.sync.dma_start(n_words[:].bitcast(I32), notes_words[0].bitcast(I32))
+        idx2 = load_list(offs2, "idx2")
         thr_sb = keep.tile([P, 1], F32, name="thr_sb")
         slope_sb = keep.tile([P, 1], F32, name="slope_sb")
         nc.sync.dma_start(slope_sb[:], slope)
-        nc.sync.dma_start(thr_sb[:], thr)
-        idx2 = load_list(offs2, "idx2")
+        nc.gpsimd.dma_start(thr_sb[:], thr)
         idx4 = load_list(offs4, "idx4")
-        k_words = keep.tile([P, T], I32, name="k_words", align_bytes=64)
-        nc.sync.dma_start(k_words[:], keys_words[0].rearrange("p n t -> p (n t)").bitcast(I32))
+        keys_i32 = keys_words[0].rearrange("p n t -> p (n t)").bitcast(I32)
+        k_words = [keep.tile([P, BANK], I32, name="k_words%d" % c, align_bytes=64) for c in range(T // BANK)]
+        nc.sync.dma_start(k_words[0][:], keys_i32[:, :BANK])
         k_plane = load_plane(keys_scales, "k_plane")
-        idx = load_list(offs, "idx")
+        nc.sync.dma_start(k_words[1][:], keys_i32[:, BANK:])
         old_sb = keep.tile([P, Z], F32, name="old_sb")
         nc.sync.dma_start(old_sb[:], old)
+        idx = load_list(offs, "idx")
         idx3 = load_list(offs3, "idx3")
         idx5 = load_list(offs5, "idx5")
 
@@ -98,7 +100,7 @@ def tile_attend_twogates_two_kernel(tc, query, keys_words, keys_scales, notes_wo
         f1 = keep.tile([P, Z], F32, name="f1", tag="q_then_f1", align_bytes=64)
         nc.gpsimd.memset(f1[:], 0.0)
 
-        b_sb = keep.tile([P, T], F32, name="b_sb", tag="rows")
+        b_sb = keep.tile([P, T], F32, name="b_sb")
         c0 = 0
         for n, width in enumerate(B_PIECES):
             acc = bank(n, "b_acc%d" % n)
@@ -119,18 +121,15 @@ def tile_attend_twogates_two_kernel(tc, query, keys_words, keys_scales, notes_wo
         a_sb = keep.tile([P, T], F32, name="a_sb", tag="rows")
         for c in range(T // BANK):
             cols = slice(c * BANK, (c + 1) * BANK)
-            acc = bank(c, "a_acc%d" % c)
+            acc = bank(3 - c, "a_acc%d" % c)
             nc.tensor.matmul_mx(out=acc[:], lhsT=q_codes[:].bitcast(FP8X4), lhsT_scale=q_plane[:],
-                                rhs=k_words[:, cols].bitcast(FP8X4), rhs_scale=k_plane[:, cols],
+                                rhs=k_words[c][:].bitcast(FP8X4), rhs_scale=k_plane[:, cols],
                                 start=True, stop=True)
             nc.scalar.copy(a_sb[:, cols], acc[:])
 
         s1 = keep.tile([P, SLOTS], F32, name="s1")
-        for h in range(2):
-            cols = slice(h * HALF, (h + 1) * HALF)
-            nc.scalar.activation(s1[:, cols], a_sb[:].indirect(half(idx, h)), ACT.Sigmoid,
-                                 bias=thr_sb[:], scale=slope_sb[:])
-            nc.vector.tensor_copy(f1[:].indirect(half(idx3, h)), s1[:, cols])
+        nc.scalar.activation(s1[:], a_sb[:].indirect(idx[:]), ACT.Sigmoid, bias=thr_sb[:], scale=slope_sb[:])
+        nc.vector.tensor_copy(f1[:].indirect(idx3[:]), s1[:])
 
         n_turn = Z // TURN
         per = TURN // P
@@ -142,7 +141,7 @@ def tile_attend_twogates_two_kernel(tc, query, keys_words, keys_scales, notes_wo
                     nc.tensor.matmul(turned[g][:, j * P:(j + 1) * P], lhsT=src[:, z0:z0 + P], rhs=ident[:],
                                      is_transpose=True, start=(n == 0 and j == 0), stop=(n == 2 and j == per - 1))
         lowered_t = keep.tile([P, Z], F32, name="lowered_t", tag="rows")
-        lowered = [bank(2 + c, "lowered%d" % c) for c in range(Z // BANK)]
+        lowered = [bank(c, "lowered%d" % c) for c in range(Z // BANK)]
         for g in range(n_turn):
             nc.scalar.copy(lowered_t[:, g * TURN:(g + 1) * TURN], turned[g][:, :TURN])
             for j in range(per):

from contextlib import ExitStack

import concourse.mybir as mybir
from concourse.masks import make_identity

D, T, Z, SLOTS, Q = 512, 1024, 1024, 512, 128
FLOPS = 2 * 2 * D * Q * T

F32 = mybir.dt.float32
BF16 = mybir.dt.bfloat16
I32 = mybir.dt.int32
U32 = mybir.dt.uint32
U16 = mybir.dt.uint16
U8 = mybir.dt.uint8
FP8X4 = mybir.dt.float8_e4m3fn_x4
FP4X4 = mybir.dt.float4_e2m1fn_x4
ACT = mybir.ActivationFunctionType
ALU = mybir.AluOpType

P = 128
PACK = 4
BANK = 512
HALF = SLOTS // 2
LIST_COLS = SLOTS // 16
B_PIECES = (256, 256, 256, 128, 128)
TURN = 256
POOL_COLS = 224


def tile_attend_twogates_two_kernel(tc, query, keys_words, keys_scales, notes_words, notes_scales,
                                     thr, slope, old, offs, offs2, offs3, offs4, offs5, out):
    nc = tc.nc
    with ExitStack() as ctx:
        lists = ctx.enter_context(tc.tile_pool(name="lists", bufs=1))
        keep = ctx.enter_context(tc.tile_pool(name="keep", bufs=1))
        psum = ctx.enter_context(tc.psum_pool(name="psum", bufs=1))

        def load_list(src, name):
            t = lists.tile([P, LIST_COLS], U16, name=name)
            nc.sync.dma_start(t[:], src)
            return t

        def load_plane(scales, name):
            plane = keep.tile([P, T], U8, name=name, align_bytes=64)
            for r in range(4):
                nc.sync.dma_start(plane[r:P:32, :].bitcast(I32), scales[0, r:16:4, :].bitcast(I32))
            return plane

        def half(offsets, h):
            return offsets[:, h * LIST_COLS // 2:(h + 1) * LIST_COLS // 2]

        def bank(b, name):
            return psum.tile([P, BANK], F32, name=name, tag="bank%d" % b)

        q_raw = keep.tile([P, PACK, Q], F32, name="q_raw")
        nc.sync.dma_start(q_raw[:], query.rearrange("(p j) q -> p j q", j=PACK))
        n_plane = load_plane(notes_scales, "n_plane")
        n_words = keep.tile([P, 2 * T], U8, name="n_words", align_bytes=64)
        nc.sync.dma_start(n_words[:].bitcast(I32), notes_words[0].bitcast(I32))
        idx2 = load_list(offs2, "idx2")
        thr_sb = keep.tile([P, 1], F32, name="thr_sb")
        slope_sb = keep.tile([P, 1], F32, name="slope_sb")
        nc.sync.dma_start(slope_sb[:], slope)
        nc.gpsimd.dma_start(thr_sb[:], thr)
        idx4 = load_list(offs4, "idx4")
        keys_i32 = keys_words[0].rearrange("p n t -> p (n t)").bitcast(I32)
        k_words = [keep.tile([P, BANK], I32, name="k_words%d" % c, align_bytes=64) for c in range(T // BANK)]
        nc.sync.dma_start(k_words[0][:], keys_i32[:, :BANK])
        k_plane = load_plane(keys_scales, "k_plane")
        nc.sync.dma_start(k_words[1][:], keys_i32[:, BANK:])
        old_sb = keep.tile([P, Z], F32, name="old_sb")
        nc.sync.dma_start(old_sb[:], old)
        idx = load_list(offs, "idx")
        idx3 = load_list(offs3, "idx3")
        idx5 = load_list(offs5, "idx5")

        warm_in = keep.tile([P, 1], F32, name="warm_in")
        warm_out = keep.tile([P, 1], F32, name="warm_out")
        nc.vector.memset(warm_in[:], 0.0)
        nc.scalar.activation(warm_out[:], warm_in[:], ACT.Sigmoid)

        minus_f2 = [keep.tile([P, Z], F32, name="minus_f2_%d" % h) for h in range(2)]
        minus_one = keep.tile([P, HALF], F32, name="minus_one")
        nc.vector.memset(minus_f2[0][:], 0.0)
        nc.vector.memset(minus_f2[1][:], 0.0)
        nc.gpsimd.memset(minus_one[:], -1.0)
        ident = keep.tile([P, P], F32, name="ident")
        make_identity(nc, ident[:])

        q_bf = keep.tile([P, Q, PACK], BF16, name="q_bf", tag="q_then_f1", align_bytes=64)
        q_codes = keep.tile([P, Q], U32, name="q_codes", align_bytes=64)
        q_plane = keep.tile([P, Q], U8, name="q_plane", align_bytes=64)
        q_halves = [slice(0, Q // 2), slice(Q // 2, Q)]
        for cols in q_halves:
            nc.vector.tensor_copy(q_bf[:, cols, :].rearrange("p (c i) j -> p c j i", i=4),
                                  q_raw[:, :, cols].rearrange("p j (c i) -> p c j i", i=4))
        for cols in q_halves:
            nc.vector.quantize_mx(out=q_codes[:, cols].bitcast(FP8X4), scales=q_plane[:, cols],
                                  in_=q_bf[:, cols, :].rearrange("p q j -> p (q j)"))
        f1 = keep.tile([P, Z], F32, name="f1", tag="q_then_f1", align_bytes=64)
        nc.gpsimd.memset(f1[:], 0.0)

        b_sb = keep.tile([P, T], F32, name="b_sb")
        c0 = 0
        for n, width in enumerate(B_PIECES):
            acc = bank(n, "b_acc%d" % n)
            nc.tensor.matmul_mx(out=acc[:, :width], lhsT=q_codes[:].bitcast(FP8X4), lhsT_scale=q_plane[:],
                                rhs=n_words[:, 2 * c0:2 * (c0 + width)].bitcast(FP4X4),
                                rhs_scale=n_plane[:, c0:c0 + width], start=True, stop=True)
            copy_out = nc.vector.tensor_copy if n % 2 == 0 else nc.scalar.copy
            copy_out(b_sb[:, c0:c0 + width], acc[:, :width])
            c0 = c0 + width

        s2 = keep.tile([P, SLOTS], F32, name="s2")
        for h in range(2):
            cols = slice(h * HALF, (h + 1) * HALF)
            nc.scalar.activation(s2[:, cols], b_sb[:].indirect(half(idx2, h)), ACT.Sigmoid,
                                 bias=thr_sb[:], scale=slope_sb[:])
            nc.vector.tensor_tensor(minus_f2[h][:].indirect(half(idx4, h)), s2[:, cols], minus_one[:], ALU.mult)

        a_sb = keep.tile([P, T], F32, name="a_sb", tag="rows")
        for c in range(T // BANK):
            cols = slice(c * BANK, (c + 1) * BANK)
            acc = bank(3 - c, "a_acc%d" % c)
            nc.tensor.matmul_mx(out=acc[:], lhsT=q_codes[:].bitcast(FP8X4), lhsT_scale=q_plane[:],
                                rhs=k_words[c][:].bitcast(FP8X4), rhs_scale=k_plane[:, cols],
                                start=True, stop=True)
            nc.scalar.copy(a_sb[:, cols], acc[:])

        s1 = keep.tile([P, SLOTS], F32, name="s1")
        nc.scalar.activation(s1[:], a_sb[:].indirect(idx[:]), ACT.Sigmoid, bias=thr_sb[:], scale=slope_sb[:])
        nc.vector.tensor_copy(f1[:].indirect(idx3[:]), s1[:])

        n_turn = Z // TURN
        per = TURN // P
        turned = [bank(8 - n_turn + g, "turned%d" % g) for g in range(n_turn)]
        for n, src in enumerate((old_sb, minus_f2[0], minus_f2[1])):
            for g in range(n_turn):
                for j in range(per):
                    z0 = g * TURN + j * P
                    nc.tensor.matmul(turned[g][:, j * P:(j + 1) * P], lhsT=src[:, z0:z0 + P], rhs=ident[:],
                                     is_transpose=True, start=(n == 0 and j == 0), stop=(n == 2 and j == per - 1))
        lowered_t = keep.tile([P, Z], F32, name="lowered_t", tag="rows")
        lowered = [bank(c, "lowered%d" % c) for c in range(Z // BANK)]
        for g in range(n_turn):
            nc.scalar.copy(lowered_t[:, g * TURN:(g + 1) * TURN], turned[g][:, :TURN])
            for j in range(per):
                z0 = g * TURN + j * P
                nc.tensor.transpose(lowered[z0 // BANK][:, z0 % BANK:z0 % BANK + P], lowered_t[:, z0:z0 + P], ident[:])

        cc = keep.tile([P, Z], F32, name="cc")
        lowered_head = keep.tile([P, POOL_COLS], F32, name="lowered_head")
        nc.scalar.copy(lowered_head[:], lowered[0][:, :POOL_COLS])
        nc.gpsimd.tensor_tensor(cc[:, :POOL_COLS], lowered_head[:], f1[:, :POOL_COLS], ALU.add)
        nc.vector.tensor_tensor(cc[:, POOL_COLS:BANK], lowered[0][:, POOL_COLS:], f1[:, POOL_COLS:BANK], ALU.add)
        nc.vector.tensor_tensor(cc[:, BANK:], lowered[1][:], f1[:, BANK:], ALU.add)

        y0 = keep.tile([P, HALF], F32, name="y0")
        nc.vector.tensor_copy(y0[:], cc[:].indirect(half(idx5, 0)))
        nc.sync.dma_start(out[:, :HALF], y0[:])
        y1 = keep.tile([P, HALF], F32, name="y1")
        nc.scalar.activation(y1[:], cc[:].indirect(half(idx5, 1)), ACT.Copy)
        nc.scalar.dma_start(out[:, HALF:], y1[:])
